import numpy as np
import ml_dtypes


def mxq(x, axis, fmt="e4m3"):
    dtype, down = {"e4m3": (ml_dtypes.float8_e4m3fn, 7), "e5m2": (ml_dtypes.float8_e5m2, 14)}[fmt]
    v = np.moveaxis(np.asarray(x, np.float32).astype(ml_dtypes.bfloat16).astype(np.float64), axis, -1)
    blocks = v.reshape(v.shape[:-1] + (-1, 32))
    amax = np.abs(blocks).max(-1, keepdims=True)
    byte = np.maximum(np.where(amax > 0, np.frexp(amax)[1] - 1 + 127, 0) - down, 1)
    scale = np.exp2(byte - 127.0)
    codes = (blocks / scale).astype(np.float32).astype(dtype).astype(np.float64)
    return np.moveaxis((codes * scale).reshape(v.shape), -1, axis)


WIDE = False


def mx_kscale(k):
    if not WIDE:
        return np.ones(k)
    levels = np.array([10, -10, 5, -5, 0])
    if k % 512:
        return np.exp2(np.random.permutation(np.resize(levels, k // 32))).repeat(32)
    a = np.empty((k // 512, 16))
    for p in range(k // 512):
        a[p, :8] = np.random.permutation(np.resize(levels, 8))
        for g in range(8):
            far = levels[np.abs(levels - a[p, g]) >= 10]
            a[p, g + 8] = far[np.random.randint(len(far))]
    return np.exp2(a.ravel()).repeat(32)


BF16 = ml_dtypes.bfloat16


def bf(x):
    return np.asarray(x, np.float32).astype(BF16)


def f64(x):
    return np.asarray(x).astype(np.float64)


E2M1 = np.array([0.0, 0.5, 1.0, 1.5, 2.0, 3.0, 4.0, 6.0, -0.0, -0.5, -1.0, -1.5, -2.0, -3.0, -4.0, -6.0])


def pack_weight(w, fmt):
    k, n = w.shape
    w = f64(bf(w)).reshape(k // 32, 32, n)
    amax = np.abs(w).max(1)
    if fmt == "e4m3":
        byte = np.frexp(amax)[1] - 1 + 127 - 7
    else:
        mant, ex = np.frexp(amax / 6.0)
        byte = np.where(mant > 0.5, ex, ex - 1) + 127
    byte = np.clip(np.where(amax > 0, byte, 1), 1, 254)
    scaled = (w * np.exp2(127.0 - byte)[:, None, :]).reshape(k, n).astype(np.float32)
    by_word = np.ascontiguousarray(scaled.reshape(k // 512, 128, 4, n).transpose(0, 1, 3, 2))
    if fmt == "e4m3":
        words = by_word.astype(ml_dtypes.float8_e4m3fn).view(np.uint8)
    else:
        c = by_word.astype(ml_dtypes.float4_e2m1fn).view(np.uint8) & 0xF
        words = c[..., 0::2] | (c[..., 1::2] << 4)
    return np.ascontiguousarray(words), np.ascontiguousarray(byte.astype(np.uint8).reshape(k // 512, 16, n))


def unpack_weight(words, scales, fmt):
    g, p, n, _ = words.shape
    if fmt == "e4m3":
        vals = np.ascontiguousarray(words).view(ml_dtypes.float8_e4m3fn).astype(np.float64)
    else:
        nib = np.empty((g, p, n, 4), np.uint8)
        nib[..., 0::2] = words & 0xF
        nib[..., 1::2] = words >> 4
        vals = E2M1[nib]
    vals = vals * np.repeat(np.exp2(scales.astype(np.float64) - 127.0), 8, axis=1)[..., None]
    return vals.transpose(0, 1, 3, 2).reshape(g * 512, n)
def pack4(w):
    words, scales = pack_weight(w, "e2m1")
    return words.reshape(words.shape[0], 128, -1), scales


def unpack4(words, scales):
    return unpack_weight(words.reshape(words.shape[0], 128, -1, 2), scales, "e2m1")


def planes(Y):
    n, m = Y.shape
    b = f64(bf(Y)).reshape(n // 32, 32, m)
    amax = np.abs(b).max(1)
    byte = np.clip(np.where(amax > 0, np.frexp(amax)[1] - 1 + 127 - 7, 1), 1, 254)
    codes = (b * np.exp2(127.0 - byte)[:, None, :]).reshape(n, m).astype(np.float32).astype(ml_dtypes.float8_e4m3fn).view(np.uint8)
    words = codes.reshape(n // 512, 128, 4, m).transpose(0, 1, 3, 2)
    return np.ascontiguousarray(words), np.ascontiguousarray(byte.astype(np.uint8).reshape(n // 512, 16, m))


U, C, K, H, N = 1024, 1536, 3072, 1024, 1024

def setup_inputs():
    s = mx_kscale(K)
    t = mx_kscale(H)
    mean = np.random.randn(U, C)
    std = 0.7 * np.exp(0.5 * np.random.randn(U, K - C))
    stats = np.concatenate([mean, std], axis=1)
    w1 = np.random.randn(K, H) / np.sqrt(K)
    b1 = 0.2 * np.random.randn(H)
    w2 = np.random.randn(H, N) * np.sqrt(2.0 / H)
    w2 = w2 - w2.mean(axis=0, keepdims=True)
    b2 = 0.5 * np.abs(np.random.randn(N))
    gain = np.exp(0.8 * np.random.randn(N))
    shift = 0.5 * gain * np.random.randn(N)
    w1_words, w1_scales = pack4(w1 / s[:, None] * t[None, :])
    w2_words, w2_scales = pack4(w2 / t[:, None])
    return {"stats": bf(stats * s[None, :]), "w1_words": w1_words, "w1_scales": w1_scales, "b1": bf(b1 * t),
            "w2_words": w2_words, "w2_scales": w2_scales, "b2": bf(b2), "gain": bf(gain), "shift": bf(shift)}

def reference(stats, w1_words, w1_scales, b1, w2_words, w2_scales, b2, gain, shift):
    W1 = unpack4(w1_words, w1_scales)
    W2 = unpack4(w2_words, w2_scales)
    h = np.maximum((mxq(f64(stats), 1, "e4m3") @ W1) + f64(b1), 0.0)
    r = np.maximum((mxq(h, 1, "e4m3") @ W2) + f64(b2), 0.0)
    y = r * f64(gain) + f64(shift)
    Y = y.T
    words, scales = planes(Y)
    return y, words, scales

@@ -1,0 +1,455 @@
+from contextlib import ExitStack
+
+import concourse.mybir as mybir
+from concourse.masks import make_identity
+
+U, K, H, N = 1024, 3072, 1024, 1024
+FLOPS = 2 * U * K * H + 2 * U * H * N
+
+F32 = mybir.dt.float32
+BF16 = mybir.dt.bfloat16
+I32 = mybir.dt.int32
+U32 = mybir.dt.uint32
+U8 = mybir.dt.uint8
+FP8X4 = mybir.dt.float8_e4m3fn_x4
+FP4X4 = mybir.dt.float4_e2m1fn_x4
+ALU = mybir.AluOpType
+ACT = mybir.ActivationFunctionType
+
+P = 128
+BANK = 512
+TILES = U // P
+CHUNKS = K // 1024
+GROUPS = 2
+HALVES = 2
+
+
+def tile_speaker_stats_embedding_planes_h1_kernel(
+    tc, stats, w1_words, w1_scales, b1, w2_words, w2_scales, b2, gain, shift, out_0, out_1, out_2
+):
+    nc = tc.nc
+    with ExitStack() as ctx:
+        keep = ctx.enter_context(tc.tile_pool(name="keep", bufs=1))
+        work = ctx.enter_context(tc.tile_pool(name="work", bufs=1))
+        psum = ctx.enter_context(tc.psum_pool(name="psum", bufs=4))
+        ctx.enter_context(tc.manual_schedule())
+
+        def kept(shape, dtype, name):
+            return keep.tile(shape, dtype, name=name, align_bytes=64)
+
+        def streamed(shape, dtype, tag, bufs):
+            return work.tile(shape, dtype, name=tag, tag=tag, bufs=bufs, align_bytes=64)
+
+        def bank(tag):
+            return psum.tile([P, BANK], F32, name=tag, tag=tag)
+
+        ident = kept([P, P], F32, "ident")
+        w1_plane_a = kept([P, 2, H], U8, "w1_plane_a")
+        w1_plane_b = kept([P, 4, H], U8, "w1_plane_b")
+        w2_plane = kept([P, 2, N], U8, "w2_plane")
+        warm = kept([P, 8], F32, "warm")
+        nc.vector.memset(w1_plane_a[:].rearrange("p g n -> p (g n)").bitcast(I32), 0)
+        nc.vector.memset(warm[:], 0.0)
+        make_identity(nc, ident[:])
+        nc.vector.memset(w1_plane_b[:].rearrange("p g n -> p (g n)").bitcast(I32), 0)
+        nc.vector.memset(w2_plane[:].rearrange("p g n -> p (g n)").bitcast(I32), 0)
+        nc.scalar.activation(out=warm[:], in_=warm[:], func=ACT.Relu)
+
+        raw = {}
+        w1 = {}
+        vec = {}
+
+        def load_stats_chunk(i, c):
+            raw[i, c] = kept([P, 1024], BF16, "raw%d_%d" % (i, c))
+            nc.sync.dma_start(out=raw[i, c][:], in_=stats[P * i : P * (i + 1), 1024 * c : 1024 * (c + 1)])
+
+        def load_stats(i):
+            raw[i] = kept([P, K], BF16, "raw%d" % i)
+            nc.sync.dma_start(out=raw[i][:], in_=stats[P * i : P * (i + 1), :])
+
+        def load_w1(c):
+            w1[c] = kept([P, 2, 2 * H], U8, "w1_%d" % c)
+            nc.sync.dma_start(
+                out=w1[c][:].bitcast(I32),
+                in_=w1_words[2 * c : 2 * c + 2].rearrange("g p n -> p g n").bitcast(I32),
+            )
+
+        def load_plane(plane, scales):
+            for r in range(4):
+                nc.sync.dma_start(
+                    out=plane[r:P:32].bitcast(I32),
+                    in_=scales[:, r:16:4, :].rearrange("g q n -> q g n").bitcast(I32),
+                )
+
+        def load_vector(name, v):
+            vec[name] = kept([P, 8], BF16, name)
+            nc.sync.dma_start(
+                out=vec[name][:].rearrange("p (g t) -> p g t", t=4),
+                in_=v.rearrange("(g p t) -> p g t", p=P, t=4),
+            )
+
+        load_stats_chunk(0, 0)
+        load_stats_chunk(0, 1)
+        load_plane(w1_plane_a, w1_scales[0:2])
+        load_w1(0)
+        load_stats_chunk(0, 2)
+        load_plane(w1_plane_b, w1_scales[2:6])
+        load_w1(1)
+        load_stats_chunk(1, 0)
+        load_stats_chunk(1, 1)
+        load_vector("b1", b1)
+        load_stats_chunk(1, 2)
+        load_w1(2)
+        load_stats(2)
+        load_stats(3)
+        w2_raw = kept([P, 2, 2 * N], U8, "w2_raw")
+        nc.sync.dma_start(out=w2_raw[:].bitcast(I32), in_=w2_words.rearrange("g p n -> p g n").bitcast(I32))
+        load_plane(w2_plane, w2_scales)
+        load_vector("b2", b2)
+        load_vector("gain", gain)
+        load_vector("shift", shift)
+        for i in range(4, TILES):
+            load_stats(i)
+
+        w2 = kept([P, 2, 2 * N], U8, "w2")
+        w2_sc = kept([P, 2, N], U8, "w2_sc")
+        b1_rows = kept([P, BANK], F32, "b1_rows")
+        y_plane = [kept([P, GROUPS, BANK], U8, "y_plane%d" % hf) for hf in range(HALVES)]
+        h_codes = [kept([P, GROUPS, BANK], U32, "h_codes%d" % hf) for hf in range(HALVES)]
+        h_plane = [kept([P, GROUPS, BANK], U8, "h_plane%d" % hf) for hf in range(HALVES)]
+
+        srt, xbank, xt, xq, xs, acc, z, hbank, ht = {}, {}, {}, {}, {}, {}, {}, {}, {}
+        acc2, r, yt, yb, ybank = {}, {}, {}, {}, {}
+
+        def permute_w2(piece):
+            if piece < 4:
+                g, grp = divmod(piece, 2)
+                cols = slice(1024 * grp, 1024 * (grp + 1))
+                nc.vector.tensor_copy(
+                    out=w2[:, g, cols].rearrange("p (t m b) -> p t m b", t=4, b=2),
+                    in_=w2_raw[:, g, cols].rearrange("p (m t b) -> p t m b", t=4, b=2),
+                )
+            else:
+                g = piece - 4
+                nc.vector.tensor_copy(
+                    out=w2_sc[:, g, :].rearrange("p (s t m) -> p s t m", s=2, t=4),
+                    in_=w2_plane[:, g, :].rearrange("p (s m t) -> p s t m", s=2, t=4),
+                )
+
+        def spread_b1():
+            spread = bank("tr")
+            words = vec["b1"][:].bitcast(F32)
+            for j in range(4):
+                nc.tensor.transpose(
+                    spread[:, P * j : P * (j + 1)], words[:, j : j + 1].to_broadcast([P, P]), ident[:]
+                )
+            nc.scalar.copy(out=b1_rows[:], in_=spread[:])
+
+        def sort_words(i):
+            srt[i] = streamed([P, K // 2], F32, "sorted", 2)
+            nc.vector.tensor_copy(
+                out=srt[i][:].rearrange("p (g u m) -> p g u m", u=2, m=P),
+                in_=raw[i][:].bitcast(F32).rearrange("p (g m u) -> p g u m", u=2, m=P),
+            )
+
+        def sort_chunk(i, c):
+            srt[i, c] = streamed([P, BANK], F32, "sorted_chunk", 3)
+            nc.vector.tensor_copy(
+                out=srt[i, c][:].rearrange("p (g u m) -> p g u m", u=2, m=P),
+                in_=raw[i, c][:].bitcast(F32).rearrange("p (g m u) -> p g u m", u=2, m=P),
+            )
+
+        def turn_stats(i, c):
+            xbank[i, c] = bank("tr")
+            for j in range(4):
+                if i == 0:
+                    g2, u = divmod(j, 2)
+                    src = raw[0, c][:].bitcast(F32)[:, 256 * g2 + u : 256 * (g2 + 1) : 2]
+                elif i == 1:
+                    src = srt[i, c][:, P * j : P * (j + 1)]
+                else:
+                    src = srt[i][:, BANK * c + P * j : BANK * c + P * (j + 1)]
+                nc.tensor.transpose(xbank[i, c][:, P * j : P * (j + 1)], src, ident[:])
+
+        def copy_stats(i, c):
+            xt[i, c] = streamed([P, 1024], BF16, "xt", 4)
+            nc.scalar.copy(
+                out=xt[i, c][:].bitcast(F32).rearrange("p (g r u) -> p g r u", g=2, u=2),
+                in_=xbank[i, c][:].rearrange("p (g u r) -> p g r u", g=2, u=2),
+            )
+
+        def quantise_stats(i, c):
+            xq[i, c] = streamed([P, 256], U32, "xq", 6)
+            xs[i, c] = streamed([P, 256], U8, "xs", 6)
+            nc.vector.quantize_mx(out=xq[i, c][:].bitcast(FP8X4), scales=xs[i, c][:], in_=xt[i, c][:])
+
+        def stage1(i, grp, passes):
+            if passes[0] == 0:
+                acc[i, grp] = bank("acc")
+            for g in passes:
+                c, g2 = divmod(g, 2)
+                nc.tensor.matmul_mx(
+                    out=acc[i, grp][:],
+                    lhsT=xq[i, c][:, P * g2 : P * (g2 + 1)].bitcast(FP8X4),
+                    lhsT_scale=xs[i, c][:, P * g2 : P * (g2 + 1)],
+                    rhs=w1[c][:, g2, 1024 * grp : 1024 * (grp + 1)].bitcast(FP4X4),
+                    rhs_scale=(w1_plane_a[:, g] if g < 2 else w1_plane_b[:, g - 2])[:, BANK * grp : BANK * (grp + 1)],
+                    start=(g == 0),
+                    stop=(g == 5),
+                )
+
+        def add_b1(i, grp):
+            z[i, grp] = streamed([P, BANK], BF16, "z", 4)
+            nc.vector.tensor_tensor(
+                out=z[i, grp][:].rearrange("p (u m e) -> p u m e", u=2, e=2),
+                in0=acc[i, grp][:].rearrange("p (m u e) -> p u m e", u=2, e=2),
+                in1=b1_rows[:].bitcast(BF16)[:, BANK * grp : BANK * (grp + 1)].rearrange(
+                    "p (u m e) -> p u m e", u=2, e=2
+                ),
+                op=ALU.add,
+            )
+
+        def turn_hidden(i, groups, tag="tr"):
+            turned = bank(tag)
+            for grp in groups:
+                hbank[i, grp] = turned[:, 2 * P * grp : 2 * P * (grp + 1)]
+                for u in range(2):
+                    nc.tensor.transpose(
+                        hbank[i, grp][:, P * u : P * (u + 1)],
+                        z[i, grp][:].bitcast(F32)[:, P * u : P * (u + 1)],
+                        ident[:],
+                    )
+
+        def relu_hidden(i, grp):
+            ht[i, grp] = streamed([P, BANK], BF16, "ht", 4)
+            nc.scalar.activation(
+                out=ht[i, grp][:].rearrange("p (r u e) -> p r u e", u=2, e=2),
+                in_=hbank[i, grp].bitcast(BF16).rearrange("p (u r e) -> p r u e", u=2, e=2),
+                func=ACT.Relu,
+            )
+
+        def quantise_hidden(i, grp):
+            hf, j = divmod(i, 4)
+            nc.vector.quantize_mx(
+                out=h_codes[hf][:, grp, P * j : P * (j + 1)].bitcast(FP8X4),
+                scales=h_plane[hf][:, grp, P * j : P * (j + 1)],
+                in_=ht[i, grp][:],
+            )
+
+        def stage2(hf, grp, t, passes=(0, 1)):
+            if passes[0] == 0:
+                acc2[hf, grp, t] = bank("acc")
+            col = BANK * grp + P * t
+            for g in passes:
+                nc.tensor.matmul_mx(
+                    out=acc2[hf, grp, t][:],
+                    lhsT=w2[:, g, 2 * col : 2 * (col + P)].bitcast(FP4X4),
+                    lhsT_scale=w2_sc[:, g, col : col + P],
+                    rhs=h_codes[hf][:, g, :].bitcast(FP8X4),
+                    rhs_scale=h_plane[hf][:, g, :],
+                    start=(g == 0),
+                    stop=(g == 1),
+                )
+
+        def relu_out(hf, grp, t, engine="scalar"):
+            r[hf, grp, t] = streamed([P, BANK], F32, "r_" + engine, 4)
+            bias = vec["b2"][:, 4 * grp + t : 4 * grp + t + 1]
+            if engine == "scalar":
+                nc.scalar.activation(out=r[hf, grp, t][:], in_=acc2[hf, grp, t][:], func=ACT.Relu, bias=bias)
+            else:
+                nc.vector.tensor_scalar(
+                    out=r[hf, grp, t][:], in0=acc2[hf, grp, t][:], scalar1=bias, scalar2=0.0, op0=ALU.add, op1=ALU.max
+                )
+
+        def scale_shift(hf, grp, t):
+            if t == 0:
+                yt[hf, grp] = streamed([P, 4, BANK], F32, "yt", 3)
+            j = 4 * grp + t
+            nc.vector.tensor_scalar(
+                out=yt[hf, grp][:, t, :],
+                in0=r[hf, grp, t][:],
+                scalar1=vec["gain"][:, j : j + 1],
+                scalar2=vec["shift"][:, j : j + 1],
+                op0=ALU.mult,
+                op1=ALU.add,
+            )
+
+        def round_out(hf, grp):
+            yb[hf, grp] = streamed([P, 4 * BANK], BF16, "yb", 2)
+            nc.vector.tensor_copy(
+                out=yb[hf, grp][:].rearrange("p (c t) -> p c t", t=4),
+                in_=yt[hf, grp][:].rearrange("p t c -> p c t"),
+            )
+
+        def quantise_out(hf, grp):
+            codes = streamed([P, BANK], U32, "y_codes", 4)
+            cols = slice(BANK * hf, BANK * (hf + 1))
+            nc.vector.quantize_mx(out=codes[:].bitcast(FP8X4), scales=y_plane[hf][:, grp, :], in_=yb[hf, grp][:])
+            nc.sync.dma_start(
+                out=out_1[grp].rearrange("p m t -> p (m t)").bitcast(I32)[:, cols], in_=codes[:].bitcast(I32)
+            )
+
+        def store_plane(hf):
+            cols = slice(BANK * hf, BANK * (hf + 1))
+            for r in range(4):
+                nc.sync.dma_start(
+                    out=out_2[:, r:16:4, cols].rearrange("g q m -> q g m").bitcast(I32),
+                    in_=y_plane[hf][r:P:32].bitcast(I32),
+                )
+
+        def turn_out(hf, grp, j, tag="tr", slots=range(4)):
+            if slots[0] == 0:
+                ybank[hf, grp, j] = bank(tag)
+            for t in slots:
+                nc.tensor.transpose(
+                    ybank[hf, grp, j][:, P * t : P * (t + 1)], yt[hf, grp][:, t, P * j : P * (j + 1)], ident[:]
+                )
+
+        def store_out(hf, grp, j, engine):
+            rows = streamed([P, BANK], F32, "rows_" + engine, 4)
+            src = ybank[hf, grp, j][:].rearrange("p (t m) -> p m t", t=4)
+            dst = rows[:].rearrange("p (m t) -> p m t", t=4)
+            if engine == "scalar":
+                nc.scalar.copy(out=dst, in_=src)
+            else:
+                nc.vector.tensor_copy(out=dst, in_=src)
+            i = 4 * hf + j
+            nc.sync.dma_start(out=out_0[P * i : P * (i + 1), BANK * grp : BANK * (grp + 1)], in_=rows[:])
+
+        def stage2_group(hf, grp):
+            for t in range(4):
+                stage2(hf, grp, t)
+                relu_out(hf, grp, t)
+                if t > 0:
+                    scale_shift(hf, grp, t - 1)
+            scale_shift(hf, grp, 3)
+
+        def finish_group(hf, grp, engines):
+            for j in range(4):
+                turn_out(hf, grp, j)
+                store_out(hf, grp, j, engines[j])
+
+        def stage1_both(passes):
+            for g in passes:
+                stage1(0, 0, [g])
+                stage1(0, 1, [g])
+
+        def stats_chunk(i, c):
+            turn_stats(i, c)
+            copy_stats(i, c)
+
+        stats_chunk(0, 0)
+        quantise_stats(0, 0)
+        stats_chunk(0, 1)
+        quantise_stats(0, 1)
+        stage1_both((0,))
+        stats_chunk(0, 2)
+        quantise_stats(0, 2)
+        stage1_both((1, 2, 3))
+        for c in range(CHUNKS):
+            sort_chunk(1, c)
+        for c in range(CHUNKS):
+            stats_chunk(1, c)
+        spread_b1()
+        stage1_both((4, 5))
+        quantise_stats(1, 0)
+        quantise_stats(1, 1)
+        quantise_stats(1, 2)
+        sort_words(2)
+        add_b1(0, 0)
+        add_b1(0, 1)
+
+        for i in range(1, TILES - 1):
+            stage1(i, 0, range(6))
+            add_b1(i, 0)
+            if i == 6:
+                round_out(0, 0)
+            for c in range(CHUNKS):
+                stats_chunk(i + 1, c)
+            turn_hidden(i - 1, (0, 1))
+            relu_hidden(i - 1, 0)
+            relu_hidden(i - 1, 1)
+            if i + 2 < TILES:
+                sort_words(i + 2)
+            stage1(i, 1, range(6))
+            for c in range(CHUNKS):
+                quantise_stats(i + 1, c)
+            quantise_hidden(i - 1, 0)
+            add_b1(i, 1)
+            quantise_hidden(i - 1, 1)
+            for piece in {1: (0,), 2: (1, 4), 3: (2, 5), 4: (3,)}.get(i, ()):
+                permute_w2(piece)
+            if i == 5:
+                stage2_group(0, 0)
+            if i == 6:
+                quantise_out(0, 0)
+                stage2_group(0, 1)
+        stage1(7, 0, range(6))
+        add_b1(7, 0)
+        turn_hidden(6, (0, 1))
+        relu_hidden(6, 0)
+        relu_hidden(6, 1)
+        round_out(0, 1)
+        for j in range(3):
+            turn_out(0, 0, j)
+        turn_hidden(7, (0,), "acc")
+        relu_hidden(7, 0)
+        stage1(7, 1, range(6))
+        quantise_hidden(6, 0)
+        quantise_hidden(6, 1)
+        store_out(0, 0, 0, "scalar")
+        store_out(0, 0, 1, "scalar")
+        quantise_out(0, 1)
+        quantise_hidden(7, 0)
+        store_plane(0)
+        add_b1(7, 1)
+        store_out(0, 0, 2, "scalar")
+        turn_out(0, 0, 3)
+        turn_out(0, 1, 0)
+        turn_hidden(7, (1,), "acc")
+        relu_hidden(7, 1)
+        store_out(0, 0, 3, "vector")
+        turn_out(0, 1, 1)
+        turn_out(0, 1, 2)
+        store_out(0, 1, 0, "vector")
+        store_out(0, 1, 1, "scalar")
+        turn_out(0, 1, 3)
+        quantise_hidden(7, 1)
+        for t in range(3):
+            stage2(1, 0, t, (0,))
+        store_out(0, 1, 2, "scalar")
+        store_out(0, 1, 3, "vector")
+        for t in range(4):
+            stage2(1, 0, t, (1,) if t < 3 else (0, 1))
+            relu_out(1, 0, t, "vector" if t == 1 else "scalar")
+        for t in range(4):
+            scale_shift(1, 0, t)
+        for t in range(3):
+            stage2(1, 1, t)
+            relu_out(1, 1, t)
+        round_out(1, 0)
+        for j in range(4):
+            turn_out(1, 0, j)
+        store_out(1, 0, 0, "scalar")
+        store_out(1, 0, 1, "scalar")
+        scale_shift(1, 1, 0)
+        scale_shift(1, 1, 1)
+        quantise_out(1, 0)
+        stage2(1, 1, 3)
+        relu_out(1, 1, 3)
+        scale_shift(1, 1, 2)
+        store_out(1, 0, 2, "vector")
+        store_out(1, 0, 3, "scalar")
+        scale_shift(1, 1, 3)
+        for j in range(3):
+            turn_out(1, 1, j, "acc", slots=range(3))
+        round_out(1, 1)
+        for j in range(3):
+            turn_out(1, 1, j, slots=range(3, 4))
+        turn_out(1, 1, 3)
+        store_out(1, 1, 0, "scalar")
+        store_out(1, 1, 1, "scalar")
+        store_out(1, 1, 2, "scalar")
+        store_out(1, 1, 3, "vector")
+        quantise_out(1, 1)
+        store_plane(1)

@@ -67,16 +67,17 @@ def tile_speaker_stats_embedding_planes_h1_kernel(
             raw[i] = kept([P, K], BF16, "raw%d" % i)
             nc.sync.dma_start(out=raw[i][:], in_=stats[P * i : P * (i + 1), :])
 
-        def load_w1(c):
-            w1[c] = kept([P, 2, 2 * H], U8, "w1_%d" % c)
+        def load_w1(first, last):
+            words = kept([P, last - first, 2 * H], U8, "w1_%d" % first)
             nc.sync.dma_start(
-                out=w1[c][:].bitcast(I32),
-                in_=w1_words[2 * c : 2 * c + 2].rearrange("g p n -> p g n").bitcast(I32),
+                out=words[:].bitcast(I32), in_=w1_words[first:last].rearrange("g p n -> p g n").bitcast(I32)
             )
+            for g in range(first, last):
+                w1[g] = words[:, g - first, :]
 
-        def load_plane(plane, scales):
+        def load_plane(plane, scales, queue=nc.sync):
             for r in range(4):
-                nc.sync.dma_start(
+                queue.dma_start(
                     out=plane[r:P:32].bitcast(I32),
                     in_=scales[:, r:16:4, :].rearrange("g q n -> q g n").bitcast(I32),
                 )
@@ -89,17 +90,18 @@ def tile_speaker_stats_embedding_planes_h1_kernel(
             )
 
         load_stats_chunk(0, 0)
-        load_stats_chunk(0, 1)
+        load_w1(0,1)
         load_plane(w1_plane_a, w1_scales[0:2])
-        load_w1(0)
+        load_stats_chunk(0, 1)
+        load_w1(1,2)
         load_stats_chunk(0, 2)
+        load_vector("b1", b1)
         load_plane(w1_plane_b, w1_scales[2:6])
-        load_w1(1)
+        load_w1(2,4)
         load_stats_chunk(1, 0)
         load_stats_chunk(1, 1)
-        load_vector("b1", b1)
         load_stats_chunk(1, 2)
-        load_w1(2)
+        load_w1(4,6)
         load_stats(2)
         load_stats(3)
         w2_raw = kept([P, 2, 2 * N], U8, "w2_raw")
@@ -126,14 +128,14 @@ def tile_speaker_stats_embedding_planes_h1_kernel(
                 g, grp = divmod(piece, 2)
                 cols = slice(1024 * grp, 1024 * (grp + 1))
                 nc.vector.tensor_copy(
-                    out=w2[:, g, cols].rearrange("p (t m b) -> p t m b", t=4, b=2),
-                    in_=w2_raw[:, g, cols].rearrange("p (m t b) -> p t m b", t=4, b=2),
+                    out=w2[:, g, cols].rearrange("p (t c i b) -> p c t i b", t=4, i=8, b=2),
+                    in_=w2_raw[:, g, cols].rearrange("p (c i t b) -> p c t i b", t=4, i=8, b=2),
                 )
             else:
                 g = piece - 4
                 nc.vector.tensor_copy(
-                    out=w2_sc[:, g, :].rearrange("p (s t m) -> p s t m", s=2, t=4),
-                    in_=w2_plane[:, g, :].rearrange("p (s m t) -> p s t m", s=2, t=4),
+                    out=w2_sc[:, g, :].rearrange("p (s t c i) -> p s c t i", s=2, t=4, i=16),
+                    in_=w2_plane[:, g, :].rearrange("p (s c i t) -> p s c t i", s=2, t=4, i=16),
                 )
 
         def spread_b1():
@@ -145,30 +147,24 @@ def tile_speaker_stats_embedding_planes_h1_kernel(
                 )
             nc.scalar.copy(out=b1_rows[:], in_=spread[:])
 
-        def sort_words(i):
-            srt[i] = streamed([P, K // 2], F32, "sorted", 2)
-            nc.vector.tensor_copy(
-                out=srt[i][:].rearrange("p (g u m) -> p g u m", u=2, m=P),
-                in_=raw[i][:].bitcast(F32).rearrange("p (g m u) -> p g u m", u=2, m=P),
-            )
 
-        def sort_chunk(i, c):
-            srt[i, c] = streamed([P, BANK], F32, "sorted_chunk", 3)
-            nc.vector.tensor_copy(
-                out=srt[i, c][:].rearrange("p (g u m) -> p g u m", u=2, m=P),
-                in_=raw[i, c][:].bitcast(F32).rearrange("p (g m u) -> p g u m", u=2, m=P),
+        def sort_chunk(i, c, engine):
+            srt[i, c] = streamed([P, BANK], F32, "sorted_" + engine, 4)
+            words = raw[i, c][:].bitcast(F32) if i < 2 else raw[i][:].bitcast(F32)[:, BANK * c : BANK * (c + 1)]
+            copy = nc.scalar.copy if engine == "scalar" else nc.vector.tensor_copy
+            copy(
+                out=srt[i, c][:].rearrange("p (g u c i) -> p g c u i", g=2, u=2, i=4),
+                in_=words.rearrange("p (g c i u) -> p g c u i", g=2, u=2, i=4),
             )
 
         def turn_stats(i, c):
             xbank[i, c] = bank("tr")
             for j in range(4):
-                if i == 0:
+                if (i, c) not in srt:
                     g2, u = divmod(j, 2)
-                    src = raw[0, c][:].bitcast(F32)[:, 256 * g2 + u : 256 * (g2 + 1) : 2]
-                elif i == 1:
-                    src = srt[i, c][:, P * j : P * (j + 1)]
+                    src = raw[i, c][:].bitcast(F32)[:, 256 * g2 + u : 256 * (g2 + 1) : 2]
                 else:
-                    src = srt[i][:, BANK * c + P * j : BANK * c + P * (j + 1)]
+                    src = srt[i, c][:, P * j : P * (j + 1)]
                 nc.tensor.transpose(xbank[i, c][:, P * j : P * (j + 1)], src, ident[:])
 
         def copy_stats(i, c):
@@ -192,7 +188,7 @@ def tile_speaker_stats_embedding_planes_h1_kernel(
                     out=acc[i, grp][:],
                     lhsT=xq[i, c][:, P * g2 : P * (g2 + 1)].bitcast(FP8X4),
                     lhsT_scale=xs[i, c][:, P * g2 : P * (g2 + 1)],
-                    rhs=w1[c][:, g2, 1024 * grp : 1024 * (grp + 1)].bitcast(FP4X4),
+                    rhs=w1[g][:, 1024 * grp : 1024 * (grp + 1)].bitcast(FP4X4),
                     rhs_scale=(w1_plane_a[:, g] if g < 2 else w1_plane_b[:, g - 2])[:, BANK * grp : BANK * (grp + 1)],
                     start=(g == 0),
                     stop=(g == 5),
@@ -277,8 +273,8 @@ def tile_speaker_stats_embedding_planes_h1_kernel(
         def round_out(hf, grp):
             yb[hf, grp] = streamed([P, 4 * BANK], BF16, "yb", 2)
             nc.vector.tensor_copy(
-                out=yb[hf, grp][:].rearrange("p (c t) -> p c t", t=4),
-                in_=yt[hf, grp][:].rearrange("p t c -> p c t"),
+                out=yb[hf, grp][:].rearrange("p (c i t) -> p c t i", t=4, i=4),
+                in_=yt[hf, grp][:].rearrange("p t (c i) -> p c t i", i=4),
             )
 
         def quantise_out(hf, grp):
@@ -339,23 +335,26 @@ def tile_speaker_stats_embedding_planes_h1_kernel(
             copy_stats(i, c)
 
         stats_chunk(0, 0)
+        sort_chunk(0, 1, "vector")
         quantise_stats(0, 0)
         stats_chunk(0, 1)
+        sort_chunk(0, 2, "vector")
         quantise_stats(0, 1)
-        stage1_both((0,))
+        stage1_both((0,1))
         stats_chunk(0, 2)
+        spread_b1()
         quantise_stats(0, 2)
-        stage1_both((1, 2, 3))
+        stage1_both((2,3))
         for c in range(CHUNKS):
-            sort_chunk(1, c)
+            sort_chunk(1, c, "vector")
         for c in range(CHUNKS):
             stats_chunk(1, c)
-        spread_b1()
         stage1_both((4, 5))
         quantise_stats(1, 0)
         quantise_stats(1, 1)
         quantise_stats(1, 2)
-        sort_words(2)
+        for c in range(CHUNKS):
+            sort_chunk(2, c, "vector" if c < 2 else "scalar")
         add_b1(0, 0)
         add_b1(0, 1)
 
@@ -370,7 +369,8 @@ def tile_speaker_stats_embedding_planes_h1_kernel(
             relu_hidden(i - 1, 0)
             relu_hidden(i - 1, 1)
             if i + 2 < TILES:
-                sort_words(i + 2)
+                for c in range(CHUNKS):
+                    sort_chunk(i + 2, c, "vector" if c < 2 else "scalar")
             stage1(i, 1, range(6))
             for c in range(CHUNKS):
                 quantise_stats(i + 1, c)
@@ -390,9 +390,9 @@ def tile_speaker_stats_embedding_planes_h1_kernel(
         relu_hidden(6, 0)
         relu_hidden(6, 1)
         round_out(0, 1)
-        for j in range(3):
+        for j in range(2):
             turn_out(0, 0, j)
-        turn_hidden(7, (0,), "acc")
+        turn_hidden(7, (0,))
         relu_hidden(7, 0)
         stage1(7, 1, range(6))
         quantise_hidden(6, 0)
@@ -403,24 +403,20 @@ def tile_speaker_stats_embedding_planes_h1_kernel(
         quantise_hidden(7, 0)
         store_plane(0)
         add_b1(7, 1)
-        store_out(0, 0, 2, "scalar")
+        turn_out(0, 0, 2)
         turn_out(0, 0, 3)
-        turn_out(0, 1, 0)
         turn_hidden(7, (1,), "acc")
+        store_out(0, 0, 2, "scalar")
         relu_hidden(7, 1)
         store_out(0, 0, 3, "vector")
-        turn_out(0, 1, 1)
-        turn_out(0, 1, 2)
-        store_out(0, 1, 0, "vector")
-        store_out(0, 1, 1, "scalar")
-        turn_out(0, 1, 3)
-        quantise_hidden(7, 1)
-        for t in range(3):
+        for t in range(2):
             stage2(1, 0, t, (0,))
-        store_out(0, 1, 2, "scalar")
-        store_out(0, 1, 3, "vector")
+        quantise_hidden(7, 1)
+        for j in range(4):
+            turn_out(0, 1, j)
+            store_out(0, 1, j, "vector" if j % 2 else "scalar")
         for t in range(4):
-            stage2(1, 0, t, (1,) if t < 3 else (0, 1))
+            stage2(1, 0, t, (1,) if t < 2 else (0, 1))
             relu_out(1, 0, t, "vector" if t == 1 else "scalar")
         for t in range(4):
             scale_shift(1, 0, t)

@@ -82,9 +82,9 @@ def tile_speaker_stats_embedding_planes_h1_kernel(
                     in_=scales[:, r:16:4, :].rearrange("g q n -> q g n").bitcast(I32),
                 )
 
-        def load_vector(name, v):
+        def load_vector(name, v, queue=nc.sync):
             vec[name] = kept([P, 8], BF16, name)
-            nc.sync.dma_start(
+            queue.dma_start(
                 out=vec[name][:].rearrange("p (g t) -> p g t", t=4),
                 in_=v.rearrange("(g p t) -> p g t", p=P, t=4),
             )
@@ -96,7 +96,7 @@ def tile_speaker_stats_embedding_planes_h1_kernel(
         load_w1(1,2)
         load_stats_chunk(0, 2)
         load_vector("b1", b1)
-        load_plane(w1_plane_b, w1_scales[2:6])
+        load_plane(w1_plane_b, w1_scales[2:6], nc.gpsimd)
         load_w1(2,4)
         load_stats_chunk(1, 0)
         load_stats_chunk(1, 1)
@@ -121,6 +121,7 @@ def tile_speaker_stats_embedding_planes_h1_kernel(
         h_plane = [kept([P, GROUPS, BANK], U8, "h_plane%d" % hf) for hf in range(HALVES)]
 
         srt, xbank, xt, xq, xs, acc, z, hbank, ht = {}, {}, {}, {}, {}, {}, {}, {}, {}
+        x_codes, x_plane = {}, {}
         acc2, r, yt, yb, ybank = {}, {}, {}, {}, {}
 
         def permute_w2(piece):
@@ -149,7 +150,7 @@ def tile_speaker_stats_embedding_planes_h1_kernel(
 
 
         def sort_chunk(i, c, engine):
-            srt[i, c] = streamed([P, BANK], F32, "sorted_" + engine, 4)
+            srt[i, c] = streamed([P, BANK], F32, "sorted_" + engine, 6)
             words = raw[i, c][:].bitcast(F32) if i < 2 else raw[i][:].bitcast(F32)[:, BANK * c : BANK * (c + 1)]
             copy = nc.scalar.copy if engine == "scalar" else nc.vector.tensor_copy
             copy(
@@ -175,19 +176,37 @@ def tile_speaker_stats_embedding_planes_h1_kernel(
             )
 
         def quantise_stats(i, c):
-            xq[i, c] = streamed([P, 256], U32, "xq", 6)
-            xs[i, c] = streamed([P, 256], U8, "xs", 6)
+            xq[i, c] = streamed([P, 256], U32, "xq", 8)
+            xs[i, c] = streamed([P, 256], U8, "xs", 8)
             nc.vector.quantize_mx(out=xq[i, c][:].bitcast(FP8X4), scales=xs[i, c][:], in_=xt[i, c][:])
+            for g2 in range(2):
+                x_codes[i, 2 * c + g2] = xq[i, c][:, P * g2 : P * (g2 + 1)]
+                x_plane[i, 2 * c + g2] = xs[i, c][:, P * g2 : P * (g2 + 1)]
+
+        def first_pass_turn(g):
+            turned = bank("tr")
+            for u in range(2):
+                nc.tensor.transpose(turned[:, P * u : P * (u + 1)], raw[0, 0][:].bitcast(F32)[:, 256 * g + u : 256 * (g + 1) : 2], ident[:])
+            xt["pass", g] = kept([P, BANK], BF16, "xt_pass%d" % g)
+            nc.scalar.copy(
+                out=xt["pass", g][:].bitcast(F32).rearrange("p (r u) -> p r u", u=2),
+                in_=turned[:, 0 : 2 * P].rearrange("p (u r) -> p r u", u=2),
+            )
+
+        def first_pass_quantise(g):
+            codes = kept([P, P], U32, "xq_pass%d" % g)
+            plane = kept([P, P], U8, "xs_pass%d" % g)
+            nc.vector.quantize_mx(out=codes[:].bitcast(FP8X4), scales=plane[:], in_=xt["pass", g][:])
+            x_codes[0, g], x_plane[0, g] = codes[:], plane[:]
 
         def stage1(i, grp, passes):
             if passes[0] == 0:
                 acc[i, grp] = bank("acc")
             for g in passes:
-                c, g2 = divmod(g, 2)
                 nc.tensor.matmul_mx(
                     out=acc[i, grp][:],
-                    lhsT=xq[i, c][:, P * g2 : P * (g2 + 1)].bitcast(FP8X4),
-                    lhsT_scale=xs[i, c][:, P * g2 : P * (g2 + 1)],
+                    lhsT=x_codes[i, g].bitcast(FP8X4),
+                    lhsT_scale=x_plane[i, g],
                     rhs=w1[g][:, 1024 * grp : 1024 * (grp + 1)].bitcast(FP4X4),
                     rhs_scale=(w1_plane_a[:, g] if g < 2 else w1_plane_b[:, g - 2])[:, BANK * grp : BANK * (grp + 1)],
                     start=(g == 0),
@@ -195,7 +214,7 @@ def tile_speaker_stats_embedding_planes_h1_kernel(
                 )
 
         def add_b1(i, grp):
-            z[i, grp] = streamed([P, BANK], BF16, "z", 4)
+            z[i, grp] = streamed([P, BANK], BF16, "z", 6)
             nc.vector.tensor_tensor(
                 out=z[i, grp][:].rearrange("p (u m e) -> p u m e", u=2, e=2),
                 in0=acc[i, grp][:].rearrange("p (m u e) -> p u m e", u=2, e=2),
@@ -285,10 +304,10 @@ def tile_speaker_stats_embedding_planes_h1_kernel(
                 out=out_1[grp].rearrange("p m t -> p (m t)").bitcast(I32)[:, cols], in_=codes[:].bitcast(I32)
             )
 
-        def store_plane(hf):
+        def store_plane(hf, queue=nc.sync):
             cols = slice(BANK * hf, BANK * (hf + 1))
             for r in range(4):
-                nc.sync.dma_start(
+                queue.dma_start(
                     out=out_2[:, r:16:4, cols].rearrange("g q m -> q g m").bitcast(I32),
                     in_=y_plane[hf][r:P:32].bitcast(I32),
                 )
@@ -334,19 +353,23 @@ def tile_speaker_stats_embedding_planes_h1_kernel(
             turn_stats(i, c)
             copy_stats(i, c)
 
-        stats_chunk(0, 0)
+        first_pass_turn(0)
+        first_pass_turn(1)
+        first_pass_quantise(0)
+        first_pass_quantise(1)
         sort_chunk(0, 1, "vector")
-        quantise_stats(0, 0)
+        stage1_both((0,))
         stats_chunk(0, 1)
         sort_chunk(0, 2, "vector")
-        quantise_stats(0, 1)
-        stage1_both((0,1))
+        stage1_both((1,))
         stats_chunk(0, 2)
         spread_b1()
+        quantise_stats(0, 1)
+        sort_chunk(1, 0, "vector")
+        sort_chunk(1, 1, "vector")
         quantise_stats(0, 2)
         stage1_both((2,3))
-        for c in range(CHUNKS):
-            sort_chunk(1, c, "vector")
+        sort_chunk(1, 2, "vector")
         for c in range(CHUNKS):
             stats_chunk(1, c)
         stage1_both((4, 5))
@@ -448,4 +471,4 @@ def tile_speaker_stats_embedding_planes_h1_kernel(
         store_out(1, 1, 2, "scalar")
         store_out(1, 1, 3, "vector")
         quantise_out(1, 1)
-        store_plane(1)
+        store_plane(1, nc.scalar)

@@ -47,13 +47,10 @@ def tile_speaker_stats_embedding_planes_h1_kernel(
         w1_plane_a = kept([P, 2, H], U8, "w1_plane_a")
         w1_plane_b = kept([P, 4, H], U8, "w1_plane_b")
         w2_plane = kept([P, 2, N], U8, "w2_plane")
-        warm = kept([P, 8], F32, "warm")
         nc.vector.memset(w1_plane_a[:].rearrange("p g n -> p (g n)").bitcast(I32), 0)
-        nc.vector.memset(warm[:], 0.0)
         make_identity(nc, ident[:])
         nc.vector.memset(w1_plane_b[:].rearrange("p g n -> p (g n)").bitcast(I32), 0)
         nc.vector.memset(w2_plane[:].rearrange("p g n -> p (g n)").bitcast(I32), 0)
-        nc.scalar.activation(out=warm[:], in_=warm[:], func=ACT.Relu)
 
         raw = {}
         w1 = {}
@@ -90,13 +87,13 @@ def tile_speaker_stats_embedding_planes_h1_kernel(
             )
 
         load_stats_chunk(0, 0)
+        load_vector("b1", b1, nc.scalar)
         load_w1(0,1)
         load_plane(w1_plane_a, w1_scales[0:2])
         load_stats_chunk(0, 1)
         load_w1(1,2)
         load_stats_chunk(0, 2)
-        load_vector("b1", b1)
-        load_plane(w1_plane_b, w1_scales[2:6], nc.gpsimd)
+        load_plane(w1_plane_b, w1_scales[2:6])
         load_w1(2,4)
         load_stats_chunk(1, 0)
         load_stats_chunk(1, 1)
@@ -115,7 +112,7 @@ def tile_speaker_stats_embedding_planes_h1_kernel(
 
         w2 = kept([P, 2, 2 * N], U8, "w2")
         w2_sc = kept([P, 2, N], U8, "w2_sc")
-        b1_rows = kept([P, BANK], F32, "b1_rows")
+        b1_rows = kept([P, H], BF16, "b1_rows")
         y_plane = [kept([P, GROUPS, BANK], U8, "y_plane%d" % hf) for hf in range(HALVES)]
         h_codes = [kept([P, GROUPS, BANK], U32, "h_codes%d" % hf) for hf in range(HALVES)]
         h_plane = [kept([P, GROUPS, BANK], U8, "h_plane%d" % hf) for hf in range(HALVES)]
@@ -146,7 +143,7 @@ def tile_speaker_stats_embedding_planes_h1_kernel(
                 nc.tensor.transpose(
                     spread[:, P * j : P * (j + 1)], words[:, j : j + 1].to_broadcast([P, P]), ident[:]
                 )
-            nc.scalar.copy(out=b1_rows[:], in_=spread[:])
+            nc.scalar.activation(out=b1_rows[:], in_=spread[:].bitcast(BF16), func=ACT.Copy)
 
 
         def sort_chunk(i, c, engine):
@@ -218,7 +215,7 @@ def tile_speaker_stats_embedding_planes_h1_kernel(
             nc.vector.tensor_tensor(
                 out=z[i, grp][:].rearrange("p (u m e) -> p u m e", u=2, e=2),
                 in0=acc[i, grp][:].rearrange("p (m u e) -> p u m e", u=2, e=2),
-                in1=b1_rows[:].bitcast(BF16)[:, BANK * grp : BANK * (grp + 1)].rearrange(
+                in1=b1_rows[:, BANK * grp : BANK * (grp + 1)].rearrange(
                     "p (u m e) -> p u m e", u=2, e=2
                 ),
                 op=ALU.add,
@@ -355,6 +352,7 @@ def tile_speaker_stats_embedding_planes_h1_kernel(
 
         first_pass_turn(0)
         first_pass_turn(1)
+        spread_b1()
         first_pass_quantise(0)
         first_pass_quantise(1)
         sort_chunk(0, 1, "vector")
@@ -363,7 +361,6 @@ def tile_speaker_stats_embedding_planes_h1_kernel(
         sort_chunk(0, 2, "vector")
         stage1_both((1,))
         stats_chunk(0, 2)
-        spread_b1()
         quantise_stats(0, 1)
         sort_chunk(1, 0, "vector")
         sort_chunk(1, 1, "vector")

from contextlib import ExitStack

import concourse.mybir as mybir
from concourse.masks import make_identity

U, K, H, N = 1024, 3072, 1024, 1024
FLOPS = 2 * U * K * H + 2 * U * H * N

F32 = mybir.dt.float32
BF16 = mybir.dt.bfloat16
I32 = mybir.dt.int32
U32 = mybir.dt.uint32
U8 = mybir.dt.uint8
FP8X4 = mybir.dt.float8_e4m3fn_x4
FP4X4 = mybir.dt.float4_e2m1fn_x4
ALU = mybir.AluOpType
ACT = mybir.ActivationFunctionType

P = 128
BANK = 512
TILES = U // P
CHUNKS = K // 1024
GROUPS = 2
HALVES = 2


def tile_speaker_stats_embedding_planes_h1_kernel(
    tc, stats, w1_words, w1_scales, b1, w2_words, w2_scales, b2, gain, shift, out_0, out_1, out_2
):
    nc = tc.nc
    with ExitStack() as ctx:
        keep = ctx.enter_context(tc.tile_pool(name="keep", bufs=1))
        work = ctx.enter_context(tc.tile_pool(name="work", bufs=1))
        psum = ctx.enter_context(tc.psum_pool(name="psum", bufs=4))
        ctx.enter_context(tc.manual_schedule())

        def kept(shape, dtype, name):
            return keep.tile(shape, dtype, name=name, align_bytes=64)

        def streamed(shape, dtype, tag, bufs):
            return work.tile(shape, dtype, name=tag, tag=tag, bufs=bufs, align_bytes=64)

        def bank(tag):
            return psum.tile([P, BANK], F32, name=tag, tag=tag)

        ident = kept([P, P], F32, "ident")
        w1_plane_a = kept([P, 2, H], U8, "w1_plane_a")
        w1_plane_b = kept([P, 4, H], U8, "w1_plane_b")
        w2_plane = kept([P, 2, N], U8, "w2_plane")
        nc.vector.memset(w1_plane_a[:].rearrange("p g n -> p (g n)").bitcast(I32), 0)
        make_identity(nc, ident[:])
        nc.vector.memset(w1_plane_b[:].rearrange("p g n -> p (g n)").bitcast(I32), 0)
        nc.vector.memset(w2_plane[:].rearrange("p g n -> p (g n)").bitcast(I32), 0)

        raw = {}
        w1 = {}
        vec = {}

        def load_stats_chunk(i, c):
            raw[i, c] = kept([P, 1024], BF16, "raw%d_%d" % (i, c))
            nc.sync.dma_start(out=raw[i, c][:], in_=stats[P * i : P * (i + 1), 1024 * c : 1024 * (c + 1)])

        def load_stats(i):
            raw[i] = kept([P, K], BF16, "raw%d" % i)
            nc.sync.dma_start(out=raw[i][:], in_=stats[P * i : P * (i + 1), :])

        def load_w1(first, last):
            words = kept([P, last - first, 2 * H], U8, "w1_%d" % first)
            nc.sync.dma_start(
                out=words[:].bitcast(I32), in_=w1_words[first:last].rearrange("g p n -> p g n").bitcast(I32)
            )
            for g in range(first, last):
                w1[g] = words[:, g - first, :]

        def load_plane(plane, scales, queue=nc.sync):
            for r in range(4):
                queue.dma_start(
                    out=plane[r:P:32].bitcast(I32),
                    in_=scales[:, r:16:4, :].rearrange("g q n -> q g n").bitcast(I32),
                )

        def load_vector(name, v, queue=nc.sync):
            vec[name] = kept([P, 8], BF16, name)
            queue.dma_start(
                out=vec[name][:].rearrange("p (g t) -> p g t", t=4),
                in_=v.rearrange("(g p t) -> p g t", p=P, t=4),
            )

        load_stats_chunk(0, 0)
        load_vector("b1", b1, nc.scalar)
        load_w1(0,1)
        load_plane(w1_plane_a, w1_scales[0:2])
        load_stats_chunk(0, 1)
        load_w1(1,2)
        load_stats_chunk(0, 2)
        load_plane(w1_plane_b, w1_scales[2:6])
        load_w1(2,4)
        load_stats_chunk(1, 0)
        load_stats_chunk(1, 1)
        load_stats_chunk(1, 2)
        load_w1(4,6)
        load_stats(2)
        load_stats(3)
        w2_raw = kept([P, 2, 2 * N], U8, "w2_raw")
        nc.sync.dma_start(out=w2_raw[:].bitcast(I32), in_=w2_words.rearrange("g p n -> p g n").bitcast(I32))
        load_plane(w2_plane, w2_scales)
        load_vector("b2", b2)
        load_vector("gain", gain)
        load_vector("shift", shift)
        for i in range(4, TILES):
            load_stats(i)

        w2 = kept([P, 2, 2 * N], U8, "w2")
        w2_sc = kept([P, 2, N], U8, "w2_sc")
        b1_rows = kept([P, H], BF16, "b1_rows")
        y_plane = [kept([P, GROUPS, BANK], U8, "y_plane%d" % hf) for hf in range(HALVES)]
        h_codes = [kept([P, GROUPS, BANK], U32, "h_codes%d" % hf) for hf in range(HALVES)]
        h_plane = [kept([P, GROUPS, BANK], U8, "h_plane%d" % hf) for hf in range(HALVES)]

        srt, xbank, xt, xq, xs, acc, z, hbank, ht = {}, {}, {}, {}, {}, {}, {}, {}, {}
        x_codes, x_plane = {}, {}
        acc2, r, yt, yb, ybank = {}, {}, {}, {}, {}

        def permute_w2(piece):
            if piece < 4:
                g, grp = divmod(piece, 2)
                cols = slice(1024 * grp, 1024 * (grp + 1))
                nc.vector.tensor_copy(
                    out=w2[:, g, cols].rearrange("p (t c i b) -> p c t i b", t=4, i=8, b=2),
                    in_=w2_raw[:, g, cols].rearrange("p (c i t b) -> p c t i b", t=4, i=8, b=2),
                )
            else:
                g = piece - 4
                nc.vector.tensor_copy(
                    out=w2_sc[:, g, :].rearrange("p (s t c i) -> p s c t i", s=2, t=4, i=16),
                    in_=w2_plane[:, g, :].rearrange("p (s c i t) -> p s c t i", s=2, t=4, i=16),
                )

        def spread_b1():
            spread = bank("tr")
            words = vec["b1"][:].bitcast(F32)
            for j in range(4):
                nc.tensor.transpose(
                    spread[:, P * j : P * (j + 1)], words[:, j : j + 1].to_broadcast([P, P]), ident[:]
                )
            nc.scalar.activation(out=b1_rows[:], in_=spread[:].bitcast(BF16), func=ACT.Copy)


        def sort_chunk(i, c, engine):
            srt[i, c] = streamed([P, BANK], F32, "sorted_" + engine, 6)
            words = raw[i, c][:].bitcast(F32) if i < 2 else raw[i][:].bitcast(F32)[:, BANK * c : BANK * (c + 1)]
            copy = nc.scalar.copy if engine == "scalar" else nc.vector.tensor_copy
            copy(
                out=srt[i, c][:].rearrange("p (g u c i) -> p g c u i", g=2, u=2, i=4),
                in_=words.rearrange("p (g c i u) -> p g c u i", g=2, u=2, i=4),
            )

        def turn_stats(i, c):
            xbank[i, c] = bank("tr")
            for j in range(4):
                if (i, c) not in srt:
                    g2, u = divmod(j, 2)
                    src = raw[i, c][:].bitcast(F32)[:, 256 * g2 + u : 256 * (g2 + 1) : 2]
                else:
                    src = srt[i, c][:, P * j : P * (j + 1)]
                nc.tensor.transpose(xbank[i, c][:, P * j : P * (j + 1)], src, ident[:])

        def copy_stats(i, c):
            xt[i, c] = streamed([P, 1024], BF16, "xt", 4)
            nc.scalar.copy(
                out=xt[i, c][:].bitcast(F32).rearrange("p (g r u) -> p g r u", g=2, u=2),
                in_=xbank[i, c][:].rearrange("p (g u r) -> p g r u", g=2, u=2),
            )

        def quantise_stats(i, c):
            xq[i, c] = streamed([P, 256], U32, "xq", 8)
            xs[i, c] = streamed([P, 256], U8, "xs", 8)
            nc.vector.quantize_mx(out=xq[i, c][:].bitcast(FP8X4), scales=xs[i, c][:], in_=xt[i, c][:])
            for g2 in range(2):
                x_codes[i, 2 * c + g2] = xq[i, c][:, P * g2 : P * (g2 + 1)]
                x_plane[i, 2 * c + g2] = xs[i, c][:, P * g2 : P * (g2 + 1)]

        def first_pass_turn(g):
            turned = bank("tr")
            for u in range(2):
                nc.tensor.transpose(turned[:, P * u : P * (u + 1)], raw[0, 0][:].bitcast(F32)[:, 256 * g + u : 256 * (g + 1) : 2], ident[:])
            xt["pass", g] = kept([P, BANK], BF16, "xt_pass%d" % g)
            nc.scalar.copy(
                out=xt["pass", g][:].bitcast(F32).rearrange("p (r u) -> p r u", u=2),
                in_=turned[:, 0 : 2 * P].rearrange("p (u r) -> p r u", u=2),
            )

        def first_pass_quantise(g):
            codes = kept([P, P], U32, "xq_pass%d" % g)
            plane = kept([P, P], U8, "xs_pass%d" % g)
            nc.vector.quantize_mx(out=codes[:].bitcast(FP8X4), scales=plane[:], in_=xt["pass", g][:])
            x_codes[0, g], x_plane[0, g] = codes[:], plane[:]

        def stage1(i, grp, passes):
            if passes[0] == 0:
                acc[i, grp] = bank("acc")
            for g in passes:
                nc.tensor.matmul_mx(
                    out=acc[i, grp][:],
                    lhsT=x_codes[i, g].bitcast(FP8X4),
                    lhsT_scale=x_plane[i, g],
                    rhs=w1[g][:, 1024 * grp : 1024 * (grp + 1)].bitcast(FP4X4),
                    rhs_scale=(w1_plane_a[:, g] if g < 2 else w1_plane_b[:, g - 2])[:, BANK * grp : BANK * (grp + 1)],
                    start=(g == 0),
                    stop=(g == 5),
                )

        def add_b1(i, grp):
            z[i, grp] = streamed([P, BANK], BF16, "z", 6)
            nc.vector.tensor_tensor(
                out=z[i, grp][:].rearrange("p (u m e) -> p u m e", u=2, e=2),
                in0=acc[i, grp][:].rearrange("p (m u e) -> p u m e", u=2, e=2),
                in1=b1_rows[:, BANK * grp : BANK * (grp + 1)].rearrange(
                    "p (u m e) -> p u m e", u=2, e=2
                ),
                op=ALU.add,
            )

        def turn_hidden(i, groups, tag="tr"):
            turned = bank(tag)
            for grp in groups:
                hbank[i, grp] = turned[:, 2 * P * grp : 2 * P * (grp + 1)]
                for u in range(2):
                    nc.tensor.transpose(
                        hbank[i, grp][:, P * u : P * (u + 1)],
                        z[i, grp][:].bitcast(F32)[:, P * u : P * (u + 1)],
                        ident[:],
                    )

        def relu_hidden(i, grp):
            ht[i, grp] = streamed([P, BANK], BF16, "ht", 4)
            nc.scalar.activation(
                out=ht[i, grp][:].rearrange("p (r u e) -> p r u e", u=2, e=2),
                in_=hbank[i, grp].bitcast(BF16).rearrange("p (u r e) -> p r u e", u=2, e=2),
                func=ACT.Relu,
            )

        def quantise_hidden(i, grp):
            hf, j = divmod(i, 4)
            nc.vector.quantize_mx(
                out=h_codes[hf][:, grp, P * j : P * (j + 1)].bitcast(FP8X4),
                scales=h_plane[hf][:, grp, P * j : P * (j + 1)],
                in_=ht[i, grp][:],
            )

        def stage2(hf, grp, t, passes=(0, 1)):
            if passes[0] == 0:
                acc2[hf, grp, t] = bank("acc")
            col = BANK * grp + P * t
            for g in passes:
                nc.tensor.matmul_mx(
                    out=acc2[hf, grp, t][:],
                    lhsT=w2[:, g, 2 * col : 2 * (col + P)].bitcast(FP4X4),
                    lhsT_scale=w2_sc[:, g, col : col + P],
                    rhs=h_codes[hf][:, g, :].bitcast(FP8X4),
                    rhs_scale=h_plane[hf][:, g, :],
                    start=(g == 0),
                    stop=(g == 1),
                )

        def relu_out(hf, grp, t, engine="scalar"):
            r[hf, grp, t] = streamed([P, BANK], F32, "r_" + engine, 4)
            bias = vec["b2"][:, 4 * grp + t : 4 * grp + t + 1]
            if engine == "scalar":
                nc.scalar.activation(out=r[hf, grp, t][:], in_=acc2[hf, grp, t][:], func=ACT.Relu, bias=bias)
            else:
                nc.vector.tensor_scalar(
                    out=r[hf, grp, t][:], in0=acc2[hf, grp, t][:], scalar1=bias, scalar2=0.0, op0=ALU.add, op1=ALU.max
                )

        def scale_shift(hf, grp, t):
            if t == 0:
                yt[hf, grp] = streamed([P, 4, BANK], F32, "yt", 3)
            j = 4 * grp + t
            nc.vector.tensor_scalar(
                out=yt[hf, grp][:, t, :],
                in0=r[hf, grp, t][:],
                scalar1=vec["gain"][:, j : j + 1],
                scalar2=vec["shift"][:, j : j + 1],
                op0=ALU.mult,
                op1=ALU.add,
            )

        def round_out(hf, grp):
            yb[hf, grp] = streamed([P, 4 * BANK], BF16, "yb", 2)
            nc.vector.tensor_copy(
                out=yb[hf, grp][:].rearrange("p (c i t) -> p c t i", t=4, i=4),
                in_=yt[hf, grp][:].rearrange("p t (c i) -> p c t i", i=4),
            )

        def quantise_out(hf, grp):
            codes = streamed([P, BANK], U32, "y_codes", 4)
            cols = slice(BANK * hf, BANK * (hf + 1))
            nc.vector.quantize_mx(out=codes[:].bitcast(FP8X4), scales=y_plane[hf][:, grp, :], in_=yb[hf, grp][:])
            nc.sync.dma_start(
                out=out_1[grp].rearrange("p m t -> p (m t)").bitcast(I32)[:, cols], in_=codes[:].bitcast(I32)
            )

        def store_plane(hf, queue=nc.sync):
            cols = slice(BANK * hf, BANK * (hf + 1))
            for r in range(4):
                queue.dma_start(
                    out=out_2[:, r:16:4, cols].rearrange("g q m -> q g m").bitcast(I32),
                    in_=y_plane[hf][r:P:32].bitcast(I32),
                )

        def turn_out(hf, grp, j, tag="tr", slots=range(4)):
            if slots[0] == 0:
                ybank[hf, grp, j] = bank(tag)
            for t in slots:
                nc.tensor.transpose(
                    ybank[hf, grp, j][:, P * t : P * (t + 1)], yt[hf, grp][:, t, P * j : P * (j + 1)], ident[:]
                )

        def store_out(hf, grp, j, engine):
            rows = streamed([P, BANK], F32, "rows_" + engine, 4)
            src = ybank[hf, grp, j][:].rearrange("p (t m) -> p m t", t=4)
            dst = rows[:].rearrange("p (m t) -> p m t", t=4)
            if engine == "scalar":
                nc.scalar.copy(out=dst, in_=src)
            else:
                nc.vector.tensor_copy(out=dst, in_=src)
            i = 4 * hf + j
            nc.sync.dma_start(out=out_0[P * i : P * (i + 1), BANK * grp : BANK * (grp + 1)], in_=rows[:])

        def stage2_group(hf, grp):
            for t in range(4):
                stage2(hf, grp, t)
                relu_out(hf, grp, t)
                if t > 0:
                    scale_shift(hf, grp, t - 1)
            scale_shift(hf, grp, 3)

        def finish_group(hf, grp, engines):
            for j in range(4):
                turn_out(hf, grp, j)
                store_out(hf, grp, j, engines[j])

        def stage1_both(passes):
            for g in passes:
                stage1(0, 0, [g])
                stage1(0, 1, [g])

        def stats_chunk(i, c):
            turn_stats(i, c)
            copy_stats(i, c)

        first_pass_turn(0)
        first_pass_turn(1)
        spread_b1()
        first_pass_quantise(0)
        first_pass_quantise(1)
        sort_chunk(0, 1, "vector")
        stage1_both((0,))
        stats_chunk(0, 1)
        sort_chunk(0, 2, "vector")
        stage1_both((1,))
        stats_chunk(0, 2)
        quantise_stats(0, 1)
        sort_chunk(1, 0, "vector")
        sort_chunk(1, 1, "vector")
        quantise_stats(0, 2)
        stage1_both((2,3))
        sort_chunk(1, 2, "vector")
        for c in range(CHUNKS):
            stats_chunk(1, c)
        stage1_both((4, 5))
        quantise_stats(1, 0)
        quantise_stats(1, 1)
        quantise_stats(1, 2)
        for c in range(CHUNKS):
            sort_chunk(2, c, "vector" if c < 2 else "scalar")
        add_b1(0, 0)
        add_b1(0, 1)

        for i in range(1, TILES - 1):
            stage1(i, 0, range(6))
            add_b1(i, 0)
            if i == 6:
                round_out(0, 0)
            for c in range(CHUNKS):
                stats_chunk(i + 1, c)
            turn_hidden(i - 1, (0, 1))
            relu_hidden(i - 1, 0)
            relu_hidden(i - 1, 1)
            if i + 2 < TILES:
                for c in range(CHUNKS):
                    sort_chunk(i + 2, c, "vector" if c < 2 else "scalar")
            stage1(i, 1, range(6))
            for c in range(CHUNKS):
                quantise_stats(i + 1, c)
            quantise_hidden(i - 1, 0)
            add_b1(i, 1)
            quantise_hidden(i - 1, 1)
            for piece in {1: (0,), 2: (1, 4), 3: (2, 5), 4: (3,)}.get(i, ()):
                permute_w2(piece)
            if i == 5:
                stage2_group(0, 0)
            if i == 6:
                quantise_out(0, 0)
                stage2_group(0, 1)
        stage1(7, 0, range(6))
        add_b1(7, 0)
        turn_hidden(6, (0, 1))
        relu_hidden(6, 0)
        relu_hidden(6, 1)
        round_out(0, 1)
        for j in range(2):
            turn_out(0, 0, j)
        turn_hidden(7, (0,))
        relu_hidden(7, 0)
        stage1(7, 1, range(6))
        quantise_hidden(6, 0)
        quantise_hidden(6, 1)
        store_out(0, 0, 0, "scalar")
        store_out(0, 0, 1, "scalar")
        quantise_out(0, 1)
        quantise_hidden(7, 0)
        store_plane(0)
        add_b1(7, 1)
        turn_out(0, 0, 2)
        turn_out(0, 0, 3)
        turn_hidden(7, (1,), "acc")
        store_out(0, 0, 2, "scalar")
        relu_hidden(7, 1)
        store_out(0, 0, 3, "vector")
        for t in range(2):
            stage2(1, 0, t, (0,))
        quantise_hidden(7, 1)
        for j in range(4):
            turn_out(0, 1, j)
            store_out(0, 1, j, "vector" if j % 2 else "scalar")
        for t in range(4):
            stage2(1, 0, t, (1,) if t < 2 else (0, 1))
            relu_out(1, 0, t, "vector" if t == 1 else "scalar")
        for t in range(4):
            scale_shift(1, 0, t)
        for t in range(3):
            stage2(1, 1, t)
            relu_out(1, 1, t)
        round_out(1, 0)
        for j in range(4):
            turn_out(1, 0, j)
        store_out(1, 0, 0, "scalar")
        store_out(1, 0, 1, "scalar")
        scale_shift(1, 1, 0)
        scale_shift(1, 1, 1)
        quantise_out(1, 0)
        stage2(1, 1, 3)
        relu_out(1, 1, 3)
        scale_shift(1, 1, 2)
        store_out(1, 0, 2, "vector")
        store_out(1, 0, 3, "scalar")
        scale_shift(1, 1, 3)
        for j in range(3):
            turn_out(1, 1, j, "acc", slots=range(3))
        round_out(1, 1)
        for j in range(3):
            turn_out(1, 1, j, slots=range(3, 4))
        turn_out(1, 1, 3)
        store_out(1, 1, 0, "scalar")
        store_out(1, 1, 1, "scalar")
        store_out(1, 1, 2, "scalar")
        store_out(1, 1, 3, "vector")
        quantise_out(1, 1)
        store_plane(1, nc.scalar)
